import numpy as np
CORES = [12,28,44,60,3,19,35,51]
N = 8
GR, GC = 2, 4
L, KA, KB, F = 4, 1, 2, 128
def setup_inputs(rng):
    return {"a": rng.standard_normal((N, 128, KA * 128), dtype=np.float32), "b": rng.standard_normal((N, 128, KB * F), dtype=np.float32)}
def reference(a, b):
    A, B = a.astype(np.float64), b.astype(np.float64)
    y = np.zeros((N, 128, F))
    for i in range(GR):
        for j in range(GC):
            for k in range(L):
                At = A[i * GC + k // KA][:, 128 * (k % KA):128 * (k % KA) + 128]
                Bt = B[(k // KB) * GC + j][:, F * (k % KB):F * (k % KB) + F]
                y[i * GC + j] += At.T @ Bt
    return {"y": y.astype(np.float32 if a.dtype != np.float64 else np.float64)}

@@ -1,0 +1,122 @@
+from concourse.bass import DstId, RemoteDMATransfer
+
+GR, GC = 2, 4
+KB = 2
+W = 128
+L = GR * KB
+
+N_HOP1 = 4
+N_HOP2 = 4
+N_A = 8
+
+SCRATCH = {
+    "a_all": ("sbuf", [128, L * W], "float32"),
+    "b_all": ("sbuf", [128, L * W], "float32"),
+    "b_stage": ("dram", [KB, 128, W], "float32"),
+    "relay": ("dram", [128, W], "float32"),
+    "y_ps": ("psum", [128, W], "float32"),
+    "y_sb": ("sbuf", [128, W], "float32"),
+}
+SEMAPHORES = (["ld_stage", "ld_a", "ld_b", "relay_in", "sent", "mm", "cp", "st"]
+              + ["arr_a%d" % k for k in range(L)] + ["arr_b%d" % t for t in range(KB)])
+
+
+def _engines(mask, n, first=0, step=1):
+    allowed = [e for e in range(mask.bit_length()) if (mask >> e) & 1]
+    out = 0
+    for e in allowed[first::step][:n]:
+        out |= 1 << e
+    return out
+
+
+def _dst(topo, c):
+    rid, pid, ring = topo.addr(c)
+    return DstId(rid=rid, pnc=pid)
+
+
+def _column_mate(T, rank):
+    row, col = divmod(rank, GC)
+    return T.cores[(GR - 1 - row) * GC + col]
+
+
+def _helpers(T, topo, src, dst):
+    idle = [h for h in range(topo.CHIPS * topo.CORES_PER_CHIP)
+            if topo.chip(h) == topo.chip(src) and h != src and T.rank_of(h) is None and topo.may_write(h, dst)]
+    near = [h for h in idle if topo.die(h) == topo.die(src)]
+    far = [h for h in idle if topo.die(h) != topo.die(src)]
+    order = []
+    for n in range(len(idle)):
+        order += near[n:n + 1] + far[n:n + 1]
+    return order[:KB]
+
+
+def _helper_program(g, core, T, topo):
+    for r, src in enumerate(T.cores):
+        dst = _column_mate(T, r)
+        hs = _helpers(T, topo, src, dst)
+        if core not in hs:
+            continue
+        t = hs.index(core)
+        k = KB * (r // GC) + t
+        rid, pid, ring = topo.addr(dst)
+        g.wait_ge(T.sem.relay_in, N_HOP1)
+        g.remote_dma(out_ap=T.b_all[:, k * W:(k + 1) * W], in_ap=T.relay[:, :],
+                     remote_sem=T.sem["arr_b%d" % t], local_sem=T.sem.sent, pid=pid, routing_id=rid,
+                     dma_engine_mask=_engines(topo.mask(core, dst), N_HOP2, 0, 2))
+        g.wait_ge(T.sem.sent, N_HOP2)
+
+
+def rank_program(g, core, T, topo):
+    rank = T.rank_of(core)
+    if rank is None:
+        _helper_program(g, core, T, topo)
+        return
+    row, col = divmod(rank, GC)
+    peers = [T.cores[row * GC + k] for k in range(GC) if k != col]
+    mate = _column_mate(T, rank)
+    helpers = _helpers(T, topo, core, mate)
+    own_a = T.a_all[:, col * W:(col + 1) * W]
+    own_k = [KB * row + t for t in range(KB)]
+    far_k = [KB * (GR - 1 - row) + t for t in range(KB)]
+
+    g.sync.dma_start(T.b_stage[0], T.b[:, 0:W]).then_inc(T.sem.ld_stage, 16)
+    g.scalar.dma_start(T.b_stage[1], T.b[:, W:2 * W]).then_inc(T.sem.ld_stage, 16)
+    g.scalar.dma_start(own_a, T.a[:, :]).then_inc(T.sem.ld_a, 16)
+    g.sync.dma_start(T.b_all[:, own_k[0] * W:(own_k[-1] + 1) * W], T.b[:, :]).then_inc(T.sem.ld_b, 16)
+
+    common = topo.mask(core, peers[0])
+    for c in peers[1:] + helpers:
+        common &= topo.mask(core, c)
+
+    g.wait_ge(T.sem.ld_stage, 32)
+    g.remote_dma_fused(
+        [RemoteDMATransfer(dst_ids=[_dst(topo, h)], dma_engine_mask=_engines(common, N_HOP1, t, KB),
+                           remote_sem=T.sem.relay_in, src=T.b_stage[t], dst=T.relay[:, :])
+         for t, h in enumerate(helpers)],
+        local_sem=T.sem.sent)
+
+    g.wait_ge(T.sem.ld_a, 16)
+    g.remote_dma_fused(
+        [RemoteDMATransfer(dst_ids=[_dst(topo, c) for c in peers], dma_engine_mask=_engines(common, N_A),
+                           remote_sem=T.sem["arr_a%d" % col], srcs=[own_a], dsts=[own_a for c in peers])],
+        local_sem=T.sem.sent)
+
+    order = sorted(own_k, key=lambda k: k != col) + sorted(far_k, key=lambda k: k != col)
+    g.tensor.wait_ge(T.sem.ld_b, 16)
+    for n, k in enumerate(order):
+        if k == col:
+            g.tensor.wait_ge(T.sem.ld_a, 16)
+        else:
+            g.tensor.wait_ge(T.sem["arr_a%d" % k], N_A)
+        if k in far_k:
+            g.tensor.wait_ge(T.sem["arr_b%d" % (k % KB)], N_HOP2)
+        mm = g.tensor.matmul(T.y_ps[:, :], T.a_all[:, k * W:(k + 1) * W], T.b_all[:, k * W:(k + 1) * W],
+                             start=(n == 0), stop=(n == L - 1))
+    mm.then_inc(T.sem.mm, 1)
+
+    g.vector.wait_ge(T.sem.mm, 1)
+    g.vector.tensor_copy(T.y_sb[:, :], T.y_ps[:, :]).then_inc(T.sem.cp, 1)
+    g.sync.wait_ge(T.sem.cp, 1)
+    g.sync.dma_start(T.y[:, :], T.y_sb[:, :]).then_inc(T.sem.st, 16)
+    g.sync.wait_ge(T.sem.st, 16)
+    g.wait_ge(T.sem.sent, KB * N_HOP1 + N_A)

@@ -5,8 +5,8 @@ KB = 2
 W = 128
 L = GR * KB
 
-N_HOP1 = 4
-N_HOP2 = 4
+N_HOP1 = 8
+N_HOP2 = 8
 N_A = 8
 
 SCRATCH = {
@@ -17,8 +17,9 @@ SCRATCH = {
     "y_ps": ("psum", [128, W], "float32"),
     "y_sb": ("sbuf", [128, W], "float32"),
 }
-SEMAPHORES = (["ld_stage", "ld_a", "ld_b", "relay_in", "sent", "mm", "cp", "st"]
-              + ["arr_a%d" % k for k in range(L)] + ["arr_b%d" % t for t in range(KB)])
+SEMAPHORES = (["ld_a", "ld_b", "relay_in", "sent", "mm", "cp", "st"]
+              + ["arr_a%d" % k for k in range(L)] + ["arr_b%d" % t for t in range(KB)]
+              + ["ld_stage%d" % t for t in range(KB)])
 
 
 def _engines(mask, n, first=0, step=1):
@@ -39,6 +40,11 @@ def _column_mate(T, rank):
     return T.cores[(GR - 1 - row) * GC + col]
 
 
+def _tile_order(rank):
+    row, col = divmod(rank, GC)
+    return sorted(range(KB), key=lambda t: (KB * row + t) ^ col)
+
+
 def _helpers(T, topo, src, dst):
     idle = [h for h in range(topo.CHIPS * topo.CORES_PER_CHIP)
             if topo.chip(h) == topo.chip(src) and h != src and T.rank_of(h) is None and topo.may_write(h, dst)]
@@ -56,13 +62,13 @@ def _helper_program(g, core, T, topo):
         hs = _helpers(T, topo, src, dst)
         if core not in hs:
             continue
-        t = hs.index(core)
+        t = _tile_order(r)[hs.index(core)]
         k = KB * (r // GC) + t
         rid, pid, ring = topo.addr(dst)
         g.wait_ge(T.sem.relay_in, N_HOP1)
         g.remote_dma(out_ap=T.b_all[:, k * W:(k + 1) * W], in_ap=T.relay[:, :],
                      remote_sem=T.sem["arr_b%d" % t], local_sem=T.sem.sent, pid=pid, routing_id=rid,
-                     dma_engine_mask=_engines(topo.mask(core, dst), N_HOP2, 0, 2))
+                     dma_engine_mask=_engines(topo.mask(core, dst), N_HOP2))
         g.wait_ge(T.sem.sent, N_HOP2)
 
 
@@ -72,15 +78,16 @@ def rank_program(g, core, T, topo):
         _helper_program(g, core, T, topo)
         return
     row, col = divmod(rank, GC)
-    peers = [T.cores[row * GC + k] for k in range(GC) if k != col]
+    peers = [T.cores[row * GC + (col ^ s)] for s in range(1, GC)]
     mate = _column_mate(T, rank)
     helpers = _helpers(T, topo, core, mate)
+    tiles = _tile_order(rank)
     own_a = T.a_all[:, col * W:(col + 1) * W]
     own_k = [KB * row + t for t in range(KB)]
     far_k = [KB * (GR - 1 - row) + t for t in range(KB)]
 
-    g.sync.dma_start(T.b_stage[0], T.b[:, 0:W]).then_inc(T.sem.ld_stage, 16)
-    g.scalar.dma_start(T.b_stage[1], T.b[:, W:2 * W]).then_inc(T.sem.ld_stage, 16)
+    for q, t in zip((g.sync, g.scalar), tiles):
+        q.dma_start(T.b_stage[t], T.b[:, t * W:(t + 1) * W]).then_inc(T.sem["ld_stage%d" % t], 16)
     g.scalar.dma_start(own_a, T.a[:, :]).then_inc(T.sem.ld_a, 16)
     g.sync.dma_start(T.b_all[:, own_k[0] * W:(own_k[-1] + 1) * W], T.b[:, :]).then_inc(T.sem.ld_b, 16)
 
@@ -88,12 +95,11 @@ def rank_program(g, core, T, topo):
     for c in peers[1:] + helpers:
         common &= topo.mask(core, c)
 
-    g.wait_ge(T.sem.ld_stage, 32)
-    g.remote_dma_fused(
-        [RemoteDMATransfer(dst_ids=[_dst(topo, h)], dma_engine_mask=_engines(common, N_HOP1, t, KB),
-                           remote_sem=T.sem.relay_in, src=T.b_stage[t], dst=T.relay[:, :])
-         for t, h in enumerate(helpers)],
-        local_sem=T.sem.sent)
+    for t, h in zip(tiles, helpers):
+        rid, pid, ring = topo.addr(h)
+        g.wait_ge(T.sem["ld_stage%d" % t], 16)
+        g.remote_dma(out_ap=T.relay[:, :], in_ap=T.b_stage[t], remote_sem=T.sem.relay_in, local_sem=T.sem.sent,
+                     pid=pid, routing_id=rid, dma_engine_mask=_engines(common, N_HOP1))
 
     g.wait_ge(T.sem.ld_a, 16)
     g.remote_dma_fused(
@@ -101,7 +107,7 @@ def rank_program(g, core, T, topo):
                            remote_sem=T.sem["arr_a%d" % col], srcs=[own_a], dsts=[own_a for c in peers])],
         local_sem=T.sem.sent)
 
-    order = sorted(own_k, key=lambda k: k != col) + sorted(far_k, key=lambda k: k != col)
+    order = sorted(own_k, key=lambda k: k ^ col) + sorted(far_k, key=lambda k: k ^ col)
     g.tensor.wait_ge(T.sem.ld_b, 16)
     for n, k in enumerate(order):
         if k == col:

from concourse.bass import DstId, RemoteDMATransfer

GR, GC = 2, 4
KB = 2
W = 128
L = GR * KB

N_HOP1 = 8
N_HOP2 = 8
N_A = 8

SCRATCH = {
    "a_all": ("sbuf", [128, L * W], "float32"),
    "b_all": ("sbuf", [128, L * W], "float32"),
    "b_stage": ("dram", [KB, 128, W], "float32"),
    "relay": ("dram", [128, W], "float32"),
    "y_ps": ("psum", [128, W], "float32"),
    "y_sb": ("sbuf", [128, W], "float32"),
}
SEMAPHORES = (["ld_a", "ld_b", "relay_in", "sent", "mm", "cp", "st"]
              + ["arr_a%d" % k for k in range(L)] + ["arr_b%d" % t for t in range(KB)]
              + ["ld_stage%d" % t for t in range(KB)])


def _engines(mask, n, first=0, step=1):
    allowed = [e for e in range(mask.bit_length()) if (mask >> e) & 1]
    out = 0
    for e in allowed[first::step][:n]:
        out |= 1 << e
    return out


def _dst(topo, c):
    rid, pid, ring = topo.addr(c)
    return DstId(rid=rid, pnc=pid)


def _column_mate(T, rank):
    row, col = divmod(rank, GC)
    return T.cores[(GR - 1 - row) * GC + col]


def _tile_order(rank):
    row, col = divmod(rank, GC)
    return sorted(range(KB), key=lambda t: (KB * row + t) ^ col)


def _helpers(T, topo, src, dst):
    idle = [h for h in range(topo.CHIPS * topo.CORES_PER_CHIP)
            if topo.chip(h) == topo.chip(src) and h != src and T.rank_of(h) is None and topo.may_write(h, dst)]
    near = [h for h in idle if topo.die(h) == topo.die(src)]
    far = [h for h in idle if topo.die(h) != topo.die(src)]
    order = []
    for n in range(len(idle)):
        order += near[n:n + 1] + far[n:n + 1]
    return order[:KB]


def _helper_program(g, core, T, topo):
    for r, src in enumerate(T.cores):
        dst = _column_mate(T, r)
        hs = _helpers(T, topo, src, dst)
        if core not in hs:
            continue
        t = _tile_order(r)[hs.index(core)]
        k = KB * (r // GC) + t
        rid, pid, ring = topo.addr(dst)
        g.wait_ge(T.sem.relay_in, N_HOP1)
        g.remote_dma(out_ap=T.b_all[:, k * W:(k + 1) * W], in_ap=T.relay[:, :],
                     remote_sem=T.sem["arr_b%d" % t], local_sem=T.sem.sent, pid=pid, routing_id=rid,
                     dma_engine_mask=_engines(topo.mask(core, dst), N_HOP2))
        g.wait_ge(T.sem.sent, N_HOP2)


def rank_program(g, core, T, topo):
    rank = T.rank_of(core)
    if rank is None:
        _helper_program(g, core, T, topo)
        return
    row, col = divmod(rank, GC)
    peers = [T.cores[row * GC + (col ^ s)] for s in range(1, GC)]
    mate = _column_mate(T, rank)
    helpers = _helpers(T, topo, core, mate)
    tiles = _tile_order(rank)
    own_a = T.a_all[:, col * W:(col + 1) * W]
    own_k = [KB * row + t for t in range(KB)]
    far_k = [KB * (GR - 1 - row) + t for t in range(KB)]

    for q, t in zip((g.sync, g.scalar), tiles):
        q.dma_start(T.b_stage[t], T.b[:, t * W:(t + 1) * W]).then_inc(T.sem["ld_stage%d" % t], 16)
    g.scalar.dma_start(own_a, T.a[:, :]).then_inc(T.sem.ld_a, 16)
    g.sync.dma_start(T.b_all[:, own_k[0] * W:(own_k[-1] + 1) * W], T.b[:, :]).then_inc(T.sem.ld_b, 16)

    common = topo.mask(core, peers[0])
    for c in peers[1:] + helpers:
        common &= topo.mask(core, c)

    for t, h in zip(tiles, helpers):
        rid, pid, ring = topo.addr(h)
        g.wait_ge(T.sem["ld_stage%d" % t], 16)
        g.remote_dma(out_ap=T.relay[:, :], in_ap=T.b_stage[t], remote_sem=T.sem.relay_in, local_sem=T.sem.sent,
                     pid=pid, routing_id=rid, dma_engine_mask=_engines(common, N_HOP1))

    g.wait_ge(T.sem.ld_a, 16)
    g.remote_dma_fused(
        [RemoteDMATransfer(dst_ids=[_dst(topo, c) for c in peers], dma_engine_mask=_engines(common, N_A),
                           remote_sem=T.sem["arr_a%d" % col], srcs=[own_a], dsts=[own_a for c in peers])],
        local_sem=T.sem.sent)

    order = sorted(own_k, key=lambda k: k ^ col) + sorted(far_k, key=lambda k: k ^ col)
    g.tensor.wait_ge(T.sem.ld_b, 16)
    for n, k in enumerate(order):
        if k == col:
            g.tensor.wait_ge(T.sem.ld_a, 16)
        else:
            g.tensor.wait_ge(T.sem["arr_a%d" % k], N_A)
        if k in far_k:
            g.tensor.wait_ge(T.sem["arr_b%d" % (k % KB)], N_HOP2)
        mm = g.tensor.matmul(T.y_ps[:, :], T.a_all[:, k * W:(k + 1) * W], T.b_all[:, k * W:(k + 1) * W],
                             start=(n == 0), stop=(n == L - 1))
    mm.then_inc(T.sem.mm, 1)

    g.vector.wait_ge(T.sem.mm, 1)
    g.vector.tensor_copy(T.y_sb[:, :], T.y_ps[:, :]).then_inc(T.sem.cp, 1)
    g.sync.wait_ge(T.sem.cp, 1)
    g.sync.dma_start(T.y[:, :], T.y_sb[:, :]).then_inc(T.sem.st, 16)
    g.sync.wait_ge(T.sem.st, 16)
    g.wait_ge(T.sem.sent, KB * N_HOP1 + N_A)
